import numpy as np
import ml_dtypes


def mxq(x, axis, fmt="e4m3"):
    dtype, down = {"e4m3": (ml_dtypes.float8_e4m3fn, 7), "e5m2": (ml_dtypes.float8_e5m2, 14)}[fmt]
    v = np.moveaxis(np.asarray(x, np.float32).astype(ml_dtypes.bfloat16).astype(np.float64), axis, -1)
    blocks = v.reshape(v.shape[:-1] + (-1, 32))
    amax = np.abs(blocks).max(-1, keepdims=True)
    byte = np.maximum(np.where(amax > 0, np.frexp(amax)[1] - 1 + 127, 0) - down, 1)
    scale = np.exp2(byte - 127.0)
    codes = (blocks / scale).astype(np.float32).astype(dtype).astype(np.float64)
    return np.moveaxis((codes * scale).reshape(v.shape), -1, axis)


WIDE = False


def mx_kscale(k):
    if not WIDE:
        return np.ones(k)
    levels = np.array([10, -10, 5, -5, 0])
    if k % 512:
        return np.exp2(np.random.permutation(np.resize(levels, k // 32))).repeat(32)
    a = np.empty((k // 512, 16))
    for p in range(k // 512):
        a[p, :8] = np.random.permutation(np.resize(levels, 8))
        for g in range(8):
            far = levels[np.abs(levels - a[p, g]) >= 10]
            a[p, g + 8] = far[np.random.randint(len(far))]
    return np.exp2(a.ravel()).repeat(32)


def f64(x):
    return np.asarray(x).astype(np.float64)


def striped8(idx):
    return np.concatenate([x.reshape(-1, 16).T for x in idx]).astype(np.uint16)


def runs(offs, k):
    lists = np.stack([offs[16 * r : 16 * r + 16].T.reshape(-1) for r in range(8)]).astype(np.int64)
    return lists[np.arange(k) % 512 // 64]


def pack_weight(w):
    k, n = w.shape
    w = f64(np.asarray(w, np.float32).astype(ml_dtypes.bfloat16)).reshape(k // 32, 32, n)
    amax = np.abs(w).max(1)
    byte = np.clip(np.where(amax > 0, np.frexp(amax)[1] - 1 + 127 - 7, 1), 1, 254)
    scaled = (w * np.exp2(127.0 - byte)[:, None, :]).reshape(k, n).astype(np.float32)
    words = np.ascontiguousarray(scaled.reshape(k // 512, 128, 4, n).transpose(0, 1, 3, 2)).astype(ml_dtypes.float8_e4m3fn).view(np.uint8)
    return words, np.ascontiguousarray(byte.astype(np.uint8).reshape(k // 512, 16, n))


def unpack_weight(words, scales):
    g, p, n, _ = words.shape
    vals = np.ascontiguousarray(words).view(ml_dtypes.float8_e4m3fn).astype(np.float64) * np.repeat(np.exp2(scales.astype(np.float64) - 127.0), 8, axis=1)[..., None]
    return vals.transpose(0, 1, 3, 2).reshape(g * 512, n)


K, T, S, G, H, C, W = 512, 1024, 512, 2048, 512, 512, 256


def setup_inputs():
    n = np.random.standard_normal
    s = mx_kscale(K)[:, None]
    packed_xT = pack_weight(n((K, T)) * s)
    packed_dT = pack_weight(n((K, G)) / s)
    perm = np.stack([np.random.permutation(S) for _ in range(8)])
    return {
        "x_words": packed_xT[0],
        "x_scales": packed_xT[1],
        "d_words": packed_dT[0],
        "d_scales": packed_dT[1],
        "gs": (np.random.uniform(0.5, 1.5, (K, 1)) / s).astype(np.float32),
        "offs": striped8(np.random.randint(0, T, (8, S))),
        "k1": striped8(np.random.randint(0, G, (8, H))),
        "cand": striped8(np.random.randint(0, T, (8, C))),
        "n1": striped8(perm[:, :W]),
        "n2": striped8(perm[:, W:]),
        "n3": striped8(np.stack([np.random.permutation(S) for _ in range(8)])),
    }


def reference(x_words, x_scales, d_words, d_scales, gs, offs, k1, cand, n1, n2, n3):
    x_cand = unpack_weight(x_words, x_scales)[np.arange(K)[:, None], runs(cand, K)]
    d_k1 = unpack_weight(d_words, d_scales)[np.arange(K)[:, None], runs(k1, K)]
    xq = unpack_weight(x_words, x_scales)[np.arange(K)[:, None], runs(offs, K)]
    h = 0.0625 * (d_k1.T @ xq)
    z = f64(gs) * h
    s = 0.0625 * ((x_cand.T @ mxq(z, 0, "e4m3")))
    pa = s[np.arange(C)[:, None], runs(n1, C)]
    pb = s[np.arange(C)[:, None], runs(n2, C)]
    rb = np.minimum(pa, pb)
    ra = np.maximum(pa, pb)
    ds = np.zeros((C, S))
    ds[np.arange(C)[:, None], runs(n1, C)] = ra
    dt = ds.copy()
    dt[np.arange(C)[:, None], runs(n2, C)] = rb
    return dt - (dt[np.arange(C)[:, None], runs(n3, C)])

@@ -1,0 +1,223 @@
+from contextlib import ExitStack
+
+import concourse.mybir as mybir
+
+K, T, S, G, H, C, W = 512, 1024, 512, 2048, 512, 512, 256
+FLOPS = 2 * K * H * S + 2 * H * C * S
+
+F32 = mybir.dt.float32
+BF16 = mybir.dt.bfloat16
+I32 = mybir.dt.int32
+U32 = mybir.dt.uint32
+U16 = mybir.dt.uint16
+U8 = mybir.dt.uint8
+FP8X4 = mybir.dt.float8_e4m3fn_x4
+ALU = mybir.AluOpType
+COPY = mybir.ActivationFunctionType.Copy
+
+P = 128
+PACK = 4
+HALF = S // 2
+QUARTER = S // 4
+SIXTEENTH = 0.0625
+
+
+def deal(nc, out, in_, run):
+    nc.vector.tensor_copy(
+        out=out.rearrange("p (t c i) -> p c t i", t=PACK, i=run),
+        in_=in_.rearrange("p (c i t) -> p c t i", t=PACK, i=run),
+    )
+
+
+def place_scale_rows(queues, plane, gathered):
+    for q in range(4):
+        queues[q % len(queues)].dma_start(
+            out=plane[32 * q : 32 * q + 4, :].bitcast(I32),
+            in_=gathered[32 * q : 32 * q + 32 : 8, :].bitcast(I32),
+        )
+
+
+def tile_picked_hpqhiordd_none_p_kernel(
+    tc, x_words, x_scales, d_words, d_scales, gs, offs, k1, cand, n1, n2, n3, out
+):
+    nc = tc.nc
+    with ExitStack() as ctx:
+        keep = ctx.enter_context(tc.tile_pool(name="keep", bufs=1))
+        psum = ctx.enter_context(tc.psum_pool(name="psum", bufs=1))
+
+        def sbuf(name, shape, dtype, tag=None):
+            return keep.tile(shape, dtype, name=name, tag=tag or name, align_bytes=64)
+
+        def load_list(name, dram):
+            tile = keep.tile(list(dram.shape), U16, name=name)
+            nc.sync.dma_start(tile[:], dram)
+            return tile
+
+        xs_table = sbuf("xs_table", [P, T], U8)
+        ds_table = sbuf("ds_table", [P, G], U8)
+        first_plane = sbuf("first_plane", [P, H + S], U8)
+        cand_plane = sbuf("cand_plane", [P, C], U8)
+        xw_table = sbuf("xw_table", [P, T], U32)
+        dw_table = sbuf("dw_table", [P, G], U32)
+        gs_sb = sbuf("gs_sb", [P, PACK], F32)
+        nc.vector.memset(xs_table[:].bitcast(I32), 0)
+        nc.vector.memset(ds_table[:].bitcast(I32), 0)
+        nc.vector.memset(first_plane[:].bitcast(I32), 0)
+        nc.vector.memset(cand_plane[:].bitcast(I32), 0)
+        offs_sb = load_list("offs_sb", offs)
+        k1_sb = load_list("k1_sb", k1)
+        cand_sb = load_list("cand_sb", cand)
+        nc.sync.dma_start(out=gs_sb[:], in_=gs.rearrange("(p t) o -> p (t o)", t=PACK))
+        nc.sync.dma_start(out=xs_table[0:P:8, :].bitcast(I32), in_=x_scales[0].bitcast(I32))
+        nc.sync.dma_start(out=ds_table[0:P:8, :].bitcast(I32), in_=d_scales[0].bitcast(I32))
+        nc.sync.dma_start(out=dw_table[:].bitcast(I32), in_=d_words[0].rearrange("p n t -> p (n t)").bitcast(I32))
+        nc.sync.dma_start(out=xw_table[:].bitcast(I32), in_=x_words[0].rearrange("p n t -> p (n t)").bitcast(I32))
+        n1_sb = load_list("n1_sb", n1)
+        n2_sb = load_list("n2_sb", n2)
+        n3_sb = load_list("n3_sb", n3)
+        gain = sbuf("gain", [P, PACK], F32)
+        nc.scalar.activation(out=gain[:], in_=gs_sb[:], func=COPY, scale=SIXTEENTH)
+
+        xs_picked = sbuf("xs_picked", [P, S], U8)
+        ds_picked = sbuf("ds_picked", [P, H], U8)
+        first_staged = sbuf("first_staged", [P, H + S], U8)
+        nc.vector.tensor_copy(xs_picked[:], xs_table[:].indirect(offs_sb[:]))
+        nc.vector.tensor_copy(ds_picked[:], ds_table[:].indirect(k1_sb[:]))
+        nc.vector.tensor_copy(first_staged[:, H:].bitcast(I32), xs_picked[:].bitcast(I32))
+        deal(nc, first_staged[:, :H], ds_picked[:], 16)
+        place_scale_rows([nc.sync, nc.scalar], first_plane, first_staged)
+
+        xq = sbuf("xq", [P, S], U32)
+        dq = sbuf("dq", [P, H], U32, "picked")
+        dq_dealt = sbuf("dq_dealt", [P, H], U32)
+        nc.vector.tensor_copy(dq[:], dw_table[:].indirect(k1_sb[:]))
+        deal(nc, dq_dealt[:], dq[:], 4)
+        nc.vector.tensor_copy(xq[:, :HALF], xw_table[:].indirect(offs_sb[:, : HALF // 16]))
+
+        def first_product(bank_cols, t, j0, n):
+            nc.tensor.matmul_mx(
+                out=bank_cols,
+                lhsT=dq_dealt[:, P * t : P * (t + 1)].bitcast(FP8X4),
+                lhsT_scale=first_plane[:, P * t : P * (t + 1)],
+                rhs=xq[:, j0 : j0 + n].bitcast(FP8X4),
+                rhs_scale=first_plane[:, H + j0 : H + j0 + n],
+                start=True,
+                stop=True,
+            )
+
+        z_low = sbuf("z_low", [P, HALF, PACK], BF16)
+        z_high = sbuf("z_high", [P, HALF, PACK], BF16)
+        for pair in range(2):
+            bank = psum.tile([P, 2, HALF], F32, name="h_low%d" % pair)
+            for u in range(2):
+                first_product(bank[:, u, :], 2 * pair + u, 0, HALF)
+            for u in range(2):
+                t = 2 * pair + u
+                nc.scalar.activation(out=z_low[:, :, t], in_=bank[:, u, :], func=COPY, scale=gain[:, t : t + 1])
+
+        nc.vector.tensor_copy(xq[:, HALF:], xw_table[:].indirect(offs_sb[:, HALF // 16 :]))
+        high_banks = []
+        for c in range(2):
+            bank = psum.tile([P, PACK, QUARTER], F32, name="h_high%d" % c)
+            for t in range(PACK):
+                first_product(bank[:, t, :], t, HALF + QUARTER * c, QUARTER)
+            high_banks.append(bank)
+
+        cand_picked = sbuf("cand_picked", [P, C], U8, "picked")
+        nc.vector.tensor_copy(cand_picked[:], xs_table[:].indirect(cand_sb[:]))
+        cand_staged = sbuf("cand_staged", [P, C], U8)
+        nc.vector.tensor_copy(
+            out=cand_staged[:].bitcast(I32).rearrange("p (t g) -> p t g", t=PACK),
+            in_=cand_picked[:].bitcast(I32).rearrange("p (g t) -> p t g", t=PACK),
+        )
+        place_scale_rows([nc.sync], cand_plane, cand_staged)
+        cq = sbuf("cq", [P, C], U32, "picked")
+        cq_dealt = sbuf("cq_dealt", [P, C], U32)
+        nc.vector.tensor_copy(cq[:], xw_table[:].indirect(cand_sb[:]))
+        nc.vector.tensor_copy(
+            out=cq_dealt[:].rearrange("p (t g a) -> p g t a", t=PACK, a=4),
+            in_=cq[:].rearrange("p (g t a) -> p g t a", t=PACK, a=4),
+        )
+
+        for c in range(2):
+            nc.vector.tensor_tensor(
+                out=z_high[:, QUARTER * c : QUARTER * (c + 1), :],
+                in0=high_banks[c][:].rearrange("p t n -> p n t"),
+                in1=gain[:].unsqueeze(1).to_broadcast([P, QUARTER, PACK]),
+                op=ALU.mult,
+            )
+        zq = sbuf("zq", [P, S], U32)
+        zs = sbuf("zs", [P, S], U8)
+        nc.vector.quantize_mx(out=zq[:, :HALF].bitcast(FP8X4), scales=zs[:, :HALF], in_=z_low[:].rearrange("p n t -> p (n t)"))
+        nc.vector.quantize_mx(out=zq[:, HALF:].bitcast(FP8X4), scales=zs[:, HALF:], in_=z_high[:].rearrange("p n t -> p (n t)"))
+
+        out_rows = out.rearrange("(g t a) j -> t g a j", t=PACK, a=4)
+        pa, pb, dt = [], [], []
+
+        def second_product(bank_cols, t, cols):
+            nc.tensor.matmul_mx(
+                out=bank_cols,
+                lhsT=cq_dealt[:, P * t : P * (t + 1)].bitcast(FP8X4),
+                lhsT_scale=cand_plane[:, P * t : P * (t + 1)],
+                rhs=zq[:, cols].bitcast(FP8X4),
+                rhs_scale=zs[:, cols],
+                start=True,
+                stop=True,
+            )
+
+        def score_and_fetch(t):
+            s = sbuf("s%d" % t, [P, S], F32)
+            if t == 0:
+                low = psum.tile([P, HALF], F32, name="s_low")
+                high = psum.tile([P, HALF], F32, name="s_high")
+                second_product(low[:], t, slice(0, HALF))
+                nc.scalar.activation(out=s[:, :HALF], in_=low[:], func=COPY, scale=SIXTEENTH)
+                second_product(high[:], t, slice(HALF, S))
+                nc.vector.tensor_scalar(out=s[:, HALF:], in0=high[:], scalar1=SIXTEENTH, scalar2=None, op0=ALU.mult)
+            else:
+                bank = psum.tile([P, S], F32, name="s_bank%d" % t, tag="h_low0" if t == PACK - 1 else "s_bank%d" % t)
+                second_product(bank[:], t, slice(0, S))
+                nc.scalar.activation(out=s[:], in_=bank[:], func=COPY, scale=SIXTEENTH)
+            pa.append(sbuf("pa%d" % t, [P, W], F32))
+            pb.append(sbuf("pb%d" % t, [P, W], F32))
+            if t == 0:
+                nc.vector.tensor_copy(pa[t][:], s[:].indirect(n1_sb[:]))
+            else:
+                nc.scalar.activation(pa[t][:], s[:].indirect(n1_sb[:]), COPY)
+            nc.scalar.activation(pb[t][:], s[:].indirect(n2_sb[:]), COPY)
+            dt.append(sbuf("dt%d" % t, [P, S], F32))
+
+        def extreme(name, t, op, tag=None):
+            tile = sbuf("%s%d" % (name, t), [P, W], F32, tag)
+            nc.vector.tensor_tensor(out=tile[:], in0=pa[t][:], in1=pb[t][:], op=op)
+            return tile
+
+        def difference(t):
+            last = t == PACK - 1
+            for h in range(2):
+                cols = slice(HALF * h, HALF * (h + 1))
+                looked_up = dt[t][:].indirect(n3_sb[:, HALF // 16 * h : HALF // 16 * (h + 1)])
+                other = sbuf("other%d_%d" % (t, h), [P, HALF], F32)
+                if last and h == 0:
+                    nc.vector.tensor_copy(other[:], looked_up)
+                else:
+                    nc.scalar.activation(other[:], looked_up, COPY)
+                result = sbuf("result%d_%d" % (t, h), [P, HALF], F32)
+                (nc.vector if last else nc.gpsimd).tensor_tensor(out=result[:], in0=dt[t][:, cols], in1=other[:], op=ALU.subtract)
+                nc.sync.dma_start(out=out_rows[t][:, :, cols], in_=result[:])
+
+        for t in range(PACK):
+            score_and_fetch(t)
+        ra = extreme("ra", 0, ALU.max)
+        nc.vector.tensor_copy(dt[0][:].indirect(n1_sb[:]), ra[:])
+        for t in range(1, PACK):
+            ra = extreme("ra", t, ALU.max)
+            rb = extreme("rb", t - 1, ALU.min, "s%d" % t)
+            if t == PACK - 1:
+                rb_last = extreme("rb", t, ALU.min)
+            nc.vector.tensor_copy(dt[t][:].indirect(n1_sb[:]), ra[:])
+            nc.vector.tensor_copy(dt[t - 1][:].indirect(n2_sb[:]), rb[:])
+            if t == PACK - 1:
+                nc.vector.tensor_copy(dt[t][:].indirect(n2_sb[:]), rb_last[:])
+            difference(t - 1)
+        difference(PACK - 1)

@@ -43,6 +43,7 @@ def tile_picked_hpqhiordd_none_p_kernel(
     nc = tc.nc
     with ExitStack() as ctx:
         keep = ctx.enter_context(tc.tile_pool(name="keep", bufs=1))
+        shared = ctx.enter_context(tc.tile_pool(name="shared", bufs=1))
         psum = ctx.enter_context(tc.psum_pool(name="psum", bufs=1))
 
         def sbuf(name, shape, dtype, tag=None):
@@ -60,19 +61,20 @@ def tile_picked_hpqhiordd_none_p_kernel(
         xw_table = sbuf("xw_table", [P, T], U32)
         dw_table = sbuf("dw_table", [P, G], U32)
         gs_sb = sbuf("gs_sb", [P, PACK], F32)
-        nc.vector.memset(xs_table[:].bitcast(I32), 0)
         nc.vector.memset(ds_table[:].bitcast(I32), 0)
         nc.vector.memset(first_plane[:].bitcast(I32), 0)
         nc.vector.memset(cand_plane[:].bitcast(I32), 0)
         offs_sb = load_list("offs_sb", offs)
+        nc.sync.dma_start(
+            out=xs_table[:].bitcast(I32), in_=x_scales[0].bitcast(I32).unsqueeze(1).to_broadcast([16, 8, T // 4])
+        )
         k1_sb = load_list("k1_sb", k1)
-        cand_sb = load_list("cand_sb", cand)
-        nc.sync.dma_start(out=gs_sb[:], in_=gs.rearrange("(p t) o -> p (t o)", t=PACK))
-        nc.sync.dma_start(out=xs_table[0:P:8, :].bitcast(I32), in_=x_scales[0].bitcast(I32))
         nc.sync.dma_start(out=ds_table[0:P:8, :].bitcast(I32), in_=d_scales[0].bitcast(I32))
         nc.sync.dma_start(out=dw_table[:].bitcast(I32), in_=d_words[0].rearrange("p n t -> p (n t)").bitcast(I32))
-        nc.sync.dma_start(out=xw_table[:].bitcast(I32), in_=x_words[0].rearrange("p n t -> p (n t)").bitcast(I32))
+        nc.sync.dma_start(out=gs_sb[:], in_=gs.rearrange("(p t) o -> p (t o)", t=PACK))
         n1_sb = load_list("n1_sb", n1)
+        nc.sync.dma_start(out=xw_table[:].bitcast(I32), in_=x_words[0].rearrange("p n t -> p (n t)").bitcast(I32))
+        cand_sb = load_list("cand_sb", cand)
         n2_sb = load_list("n2_sb", n2)
         n3_sb = load_list("n3_sb", n3)
         gain = sbuf("gain", [P, PACK], F32)
@@ -85,53 +87,59 @@ def tile_picked_hpqhiordd_none_p_kernel(
         nc.vector.tensor_copy(ds_picked[:], ds_table[:].indirect(k1_sb[:]))
         nc.vector.tensor_copy(first_staged[:, H:].bitcast(I32), xs_picked[:].bitcast(I32))
         deal(nc, first_staged[:, :H], ds_picked[:], 16)
-        place_scale_rows([nc.sync, nc.scalar], first_plane, first_staged)
+        place_scale_rows([nc.sync], first_plane, first_staged)
 
-        xq = sbuf("xq", [P, S], U32)
-        dq = sbuf("dq", [P, H], U32, "picked")
+        xq_low = sbuf("xq_low", [P, HALF], U32)
+        dq = shared.tile([P, H], U32, name="dq", offset=2048, align_bytes=64)
         dq_dealt = sbuf("dq_dealt", [P, H], U32)
         nc.vector.tensor_copy(dq[:], dw_table[:].indirect(k1_sb[:]))
+        nc.vector.tensor_copy(xq_low[:], xw_table[:].indirect(offs_sb[:, : HALF // 16]))
         deal(nc, dq_dealt[:], dq[:], 4)
-        nc.vector.tensor_copy(xq[:, :HALF], xw_table[:].indirect(offs_sb[:, : HALF // 16]))
 
-        def first_product(bank_cols, t, j0, n):
+        def first_product(bank_cols, t, xq, j0, n):
             nc.tensor.matmul_mx(
                 out=bank_cols,
                 lhsT=dq_dealt[:, P * t : P * (t + 1)].bitcast(FP8X4),
                 lhsT_scale=first_plane[:, P * t : P * (t + 1)],
-                rhs=xq[:, j0 : j0 + n].bitcast(FP8X4),
+                rhs=xq[:, j0 % HALF : j0 % HALF + n].bitcast(FP8X4),
                 rhs_scale=first_plane[:, H + j0 : H + j0 + n],
                 start=True,
                 stop=True,
             )
 
         z_low = sbuf("z_low", [P, HALF, PACK], BF16)
-        z_high = sbuf("z_high", [P, HALF, PACK], BF16)
+        z_low_rows = sbuf("z_low_rows", [P, PACK, HALF], BF16)
         for pair in range(2):
             bank = psum.tile([P, 2, HALF], F32, name="h_low%d" % pair)
             for u in range(2):
-                first_product(bank[:, u, :], 2 * pair + u, 0, HALF)
+                first_product(bank[:, u, :], 2 * pair + u, xq_low, 0, HALF)
             for u in range(2):
                 t = 2 * pair + u
-                nc.scalar.activation(out=z_low[:, :, t], in_=bank[:, u, :], func=COPY, scale=gain[:, t : t + 1])
+                nc.scalar.activation(out=z_low_rows[:, t, :], in_=bank[:, u, :], func=COPY, scale=gain[:, t : t + 1])
+        nc.scalar.copy(out=z_low[:], in_=z_low_rows[:].rearrange("p t n -> p n t"))
 
-        nc.vector.tensor_copy(xq[:, HALF:], xw_table[:].indirect(offs_sb[:, HALF // 16 :]))
+        cand_picked = [
+            shared.tile([P, C // 2], U8, name="cand_picked%d" % h, offset=2048 + 256 * h, align_bytes=64) for h in range(2)
+        ]
+        for h in range(2):
+            nc.vector.tensor_copy(cand_picked[h][:], xs_table[:].indirect(cand_sb[:, 16 * h : 16 * (h + 1)]))
+        cand_staged = sbuf("cand_staged", [P, C], U8)
+        for h in range(2):
+            nc.vector.tensor_copy(
+                out=cand_staged[:].bitcast(I32).rearrange("p (t h g) -> p h t g", t=PACK, h=2)[:, h],
+                in_=cand_picked[h][:].bitcast(I32).rearrange("p (g t) -> p t g", t=PACK),
+            )
+        place_scale_rows([nc.sync], cand_plane, cand_staged)
+        xq_high = shared.tile([P, HALF], U32, name="xq_high", offset=2560, align_bytes=64)
+        nc.vector.tensor_copy(xq_high[:], xw_table[:].indirect(offs_sb[:, HALF // 16 :]))
         high_banks = []
         for c in range(2):
             bank = psum.tile([P, PACK, QUARTER], F32, name="h_high%d" % c)
             for t in range(PACK):
-                first_product(bank[:, t, :], t, HALF + QUARTER * c, QUARTER)
+                first_product(bank[:, t, :], t, xq_high, HALF + QUARTER * c, QUARTER)
             high_banks.append(bank)
 
-        cand_picked = sbuf("cand_picked", [P, C], U8, "picked")
-        nc.vector.tensor_copy(cand_picked[:], xs_table[:].indirect(cand_sb[:]))
-        cand_staged = sbuf("cand_staged", [P, C], U8)
-        nc.vector.tensor_copy(
-            out=cand_staged[:].bitcast(I32).rearrange("p (t g) -> p t g", t=PACK),
-            in_=cand_picked[:].bitcast(I32).rearrange("p (g t) -> p t g", t=PACK),
-        )
-        place_scale_rows([nc.sync], cand_plane, cand_staged)
-        cq = sbuf("cq", [P, C], U32, "picked")
+        cq = shared.tile([P, C], U32, name="cq", offset=256, align_bytes=64)
         cq_dealt = sbuf("cq_dealt", [P, C], U32)
         nc.vector.tensor_copy(cq[:], xw_table[:].indirect(cand_sb[:]))
         nc.vector.tensor_copy(
@@ -139,17 +147,23 @@ def tile_picked_hpqhiordd_none_p_kernel(
             in_=cq[:].rearrange("p (g t a) -> p g t a", t=PACK, a=4),
         )
 
-        for c in range(2):
-            nc.vector.tensor_tensor(
-                out=z_high[:, QUARTER * c : QUARTER * (c + 1), :],
-                in0=high_banks[c][:].rearrange("p t n -> p n t"),
-                in1=gain[:].unsqueeze(1).to_broadcast([P, QUARTER, PACK]),
-                op=ALU.mult,
-            )
+        z_third = sbuf("z_third", [P, QUARTER, PACK], BF16)
+        nc.vector.tensor_tensor(
+            out=z_third[:],
+            in0=high_banks[0][:].rearrange("p t n -> p n t"),
+            in1=gain[:].unsqueeze(1).to_broadcast([P, QUARTER, PACK]),
+            op=ALU.mult,
+        )
+        z_last_rows = sbuf("z_last_rows", [P, PACK, QUARTER], BF16)
+        z_last = sbuf("z_last", [P, QUARTER, PACK], BF16)
+        for t in range(PACK):
+            nc.scalar.activation(out=z_last_rows[:, t, :], in_=high_banks[1][:, t, :], func=COPY, scale=gain[:, t : t + 1])
+        nc.scalar.copy(out=z_last[:], in_=z_last_rows[:].rearrange("p t n -> p n t"))
         zq = sbuf("zq", [P, S], U32)
         zs = sbuf("zs", [P, S], U8)
-        nc.vector.quantize_mx(out=zq[:, :HALF].bitcast(FP8X4), scales=zs[:, :HALF], in_=z_low[:].rearrange("p n t -> p (n t)"))
-        nc.vector.quantize_mx(out=zq[:, HALF:].bitcast(FP8X4), scales=zs[:, HALF:], in_=z_high[:].rearrange("p n t -> p (n t)"))
+        pieces = [(z_low, slice(0, HALF)), (z_third, slice(HALF, HALF + QUARTER)), (z_last, slice(HALF + QUARTER, S))]
+        for z, cols in pieces:
+            nc.vector.quantize_mx(out=zq[:, cols].bitcast(FP8X4), scales=zs[:, cols], in_=z[:].rearrange("p n t -> p (n t)"))
 
         out_rows = out.rearrange("(g t a) j -> t g a j", t=PACK, a=4)
         pa, pb, dt = [], [], []
@@ -168,14 +182,15 @@ def tile_picked_hpqhiordd_none_p_kernel(
         def score_and_fetch(t):
             s = sbuf("s%d" % t, [P, S], F32)
             if t == 0:
-                low = psum.tile([P, HALF], F32, name="s_low")
-                high = psum.tile([P, HALF], F32, name="s_high")
-                second_product(low[:], t, slice(0, HALF))
-                nc.scalar.activation(out=s[:, :HALF], in_=low[:], func=COPY, scale=SIXTEENTH)
-                second_product(high[:], t, slice(HALF, S))
-                nc.vector.tensor_scalar(out=s[:, HALF:], in0=high[:], scalar1=SIXTEENTH, scalar2=None, op0=ALU.mult)
+                for i, (z, cols) in enumerate(pieces):
+                    bank = psum.tile([P, cols.stop - cols.start], F32, name="s_piece%d" % i)
+                    second_product(bank[:], t, cols)
+                    if i == 0:
+                        nc.scalar.activation(out=s[:, cols], in_=bank[:], func=COPY, scale=SIXTEENTH)
+                    else:
+                        nc.vector.tensor_scalar(out=s[:, cols], in0=bank[:], scalar1=SIXTEENTH, scalar2=None, op0=ALU.mult)
             else:
-                bank = psum.tile([P, S], F32, name="s_bank%d" % t, tag="h_low0" if t == PACK - 1 else "s_bank%d" % t)
+                bank = psum.tile([P, S], F32, name="s_bank%d" % t, tag="s_bank1" if t == 1 else "h_low%d" % (t - 2))
                 second_product(bank[:], t, slice(0, S))
                 nc.scalar.activation(out=s[:], in_=bank[:], func=COPY, scale=SIXTEENTH)
             pa.append(sbuf("pa%d" % t, [P, W], F32))

from contextlib import ExitStack

import concourse.mybir as mybir

K, T, S, G, H, C, W = 512, 1024, 512, 2048, 512, 512, 256
FLOPS = 2 * K * H * S + 2 * H * C * S

F32 = mybir.dt.float32
BF16 = mybir.dt.bfloat16
I32 = mybir.dt.int32
U32 = mybir.dt.uint32
U16 = mybir.dt.uint16
U8 = mybir.dt.uint8
FP8X4 = mybir.dt.float8_e4m3fn_x4
ALU = mybir.AluOpType
COPY = mybir.ActivationFunctionType.Copy

P = 128
PACK = 4
HALF = S // 2
QUARTER = S // 4
SIXTEENTH = 0.0625


def deal(nc, out, in_, run):
    nc.vector.tensor_copy(
        out=out.rearrange("p (t c i) -> p c t i", t=PACK, i=run),
        in_=in_.rearrange("p (c i t) -> p c t i", t=PACK, i=run),
    )


def place_scale_rows(queues, plane, gathered):
    for q in range(4):
        queues[q % len(queues)].dma_start(
            out=plane[32 * q : 32 * q + 4, :].bitcast(I32),
            in_=gathered[32 * q : 32 * q + 32 : 8, :].bitcast(I32),
        )


def tile_picked_hpqhiordd_none_p_kernel(
    tc, x_words, x_scales, d_words, d_scales, gs, offs, k1, cand, n1, n2, n3, out
):
    nc = tc.nc
    with ExitStack() as ctx:
        keep = ctx.enter_context(tc.tile_pool(name="keep", bufs=1))
        shared = ctx.enter_context(tc.tile_pool(name="shared", bufs=1))
        psum = ctx.enter_context(tc.psum_pool(name="psum", bufs=1))

        def sbuf(name, shape, dtype, tag=None):
            return keep.tile(shape, dtype, name=name, tag=tag or name, align_bytes=64)

        def load_list(name, dram):
            tile = keep.tile(list(dram.shape), U16, name=name)
            nc.sync.dma_start(tile[:], dram)
            return tile

        xs_table = sbuf("xs_table", [P, T], U8)
        ds_table = sbuf("ds_table", [P, G], U8)
        first_plane = sbuf("first_plane", [P, H + S], U8)
        cand_plane = sbuf("cand_plane", [P, C], U8)
        xw_table = sbuf("xw_table", [P, T], U32)
        dw_table = sbuf("dw_table", [P, G], U32)
        gs_sb = sbuf("gs_sb", [P, PACK], F32)
        nc.vector.memset(ds_table[:].bitcast(I32), 0)
        nc.vector.memset(first_plane[:].bitcast(I32), 0)
        nc.vector.memset(cand_plane[:].bitcast(I32), 0)
        offs_sb = load_list("offs_sb", offs)
        nc.sync.dma_start(
            out=xs_table[:].bitcast(I32), in_=x_scales[0].bitcast(I32).unsqueeze(1).to_broadcast([16, 8, T // 4])
        )
        k1_sb = load_list("k1_sb", k1)
        nc.sync.dma_start(out=ds_table[0:P:8, :].bitcast(I32), in_=d_scales[0].bitcast(I32))
        nc.sync.dma_start(out=dw_table[:].bitcast(I32), in_=d_words[0].rearrange("p n t -> p (n t)").bitcast(I32))
        nc.sync.dma_start(out=gs_sb[:], in_=gs.rearrange("(p t) o -> p (t o)", t=PACK))
        n1_sb = load_list("n1_sb", n1)
        nc.sync.dma_start(out=xw_table[:].bitcast(I32), in_=x_words[0].rearrange("p n t -> p (n t)").bitcast(I32))
        cand_sb = load_list("cand_sb", cand)
        n2_sb = load_list("n2_sb", n2)
        n3_sb = load_list("n3_sb", n3)
        gain = sbuf("gain", [P, PACK], F32)
        nc.scalar.activation(out=gain[:], in_=gs_sb[:], func=COPY, scale=SIXTEENTH)

        xs_picked = sbuf("xs_picked", [P, S], U8)
        ds_picked = sbuf("ds_picked", [P, H], U8)
        first_staged = sbuf("first_staged", [P, H + S], U8)
        nc.vector.tensor_copy(xs_picked[:], xs_table[:].indirect(offs_sb[:]))
        nc.vector.tensor_copy(ds_picked[:], ds_table[:].indirect(k1_sb[:]))
        nc.vector.tensor_copy(first_staged[:, H:].bitcast(I32), xs_picked[:].bitcast(I32))
        deal(nc, first_staged[:, :H], ds_picked[:], 16)
        place_scale_rows([nc.sync], first_plane, first_staged)

        xq_low = sbuf("xq_low", [P, HALF], U32)
        dq = shared.tile([P, H], U32, name="dq", offset=2048, align_bytes=64)
        dq_dealt = sbuf("dq_dealt", [P, H], U32)
        nc.vector.tensor_copy(dq[:], dw_table[:].indirect(k1_sb[:]))
        nc.vector.tensor_copy(xq_low[:], xw_table[:].indirect(offs_sb[:, : HALF // 16]))
        deal(nc, dq_dealt[:], dq[:], 4)

        def first_product(bank_cols, t, xq, j0, n):
            nc.tensor.matmul_mx(
                out=bank_cols,
                lhsT=dq_dealt[:, P * t : P * (t + 1)].bitcast(FP8X4),
                lhsT_scale=first_plane[:, P * t : P * (t + 1)],
                rhs=xq[:, j0 % HALF : j0 % HALF + n].bitcast(FP8X4),
                rhs_scale=first_plane[:, H + j0 : H + j0 + n],
                start=True,
                stop=True,
            )

        z_low = sbuf("z_low", [P, HALF, PACK], BF16)
        z_low_rows = sbuf("z_low_rows", [P, PACK, HALF], BF16)
        for pair in range(2):
            bank = psum.tile([P, 2, HALF], F32, name="h_low%d" % pair)
            for u in range(2):
                first_product(bank[:, u, :], 2 * pair + u, xq_low, 0, HALF)
            for u in range(2):
                t = 2 * pair + u
                nc.scalar.activation(out=z_low_rows[:, t, :], in_=bank[:, u, :], func=COPY, scale=gain[:, t : t + 1])
        nc.scalar.copy(out=z_low[:], in_=z_low_rows[:].rearrange("p t n -> p n t"))

        cand_picked = [
            shared.tile([P, C // 2], U8, name="cand_picked%d" % h, offset=2048 + 256 * h, align_bytes=64) for h in range(2)
        ]
        for h in range(2):
            nc.vector.tensor_copy(cand_picked[h][:], xs_table[:].indirect(cand_sb[:, 16 * h : 16 * (h + 1)]))
        cand_staged = sbuf("cand_staged", [P, C], U8)
        for h in range(2):
            nc.vector.tensor_copy(
                out=cand_staged[:].bitcast(I32).rearrange("p (t h g) -> p h t g", t=PACK, h=2)[:, h],
                in_=cand_picked[h][:].bitcast(I32).rearrange("p (g t) -> p t g", t=PACK),
            )
        place_scale_rows([nc.sync], cand_plane, cand_staged)
        xq_high = shared.tile([P, HALF], U32, name="xq_high", offset=2560, align_bytes=64)
        nc.vector.tensor_copy(xq_high[:], xw_table[:].indirect(offs_sb[:, HALF // 16 :]))
        high_banks = []
        for c in range(2):
            bank = psum.tile([P, PACK, QUARTER], F32, name="h_high%d" % c)
            for t in range(PACK):
                first_product(bank[:, t, :], t, xq_high, HALF + QUARTER * c, QUARTER)
            high_banks.append(bank)

        cq = shared.tile([P, C], U32, name="cq", offset=256, align_bytes=64)
        cq_dealt = sbuf("cq_dealt", [P, C], U32)
        nc.vector.tensor_copy(cq[:], xw_table[:].indirect(cand_sb[:]))
        nc.vector.tensor_copy(
            out=cq_dealt[:].rearrange("p (t g a) -> p g t a", t=PACK, a=4),
            in_=cq[:].rearrange("p (g t a) -> p g t a", t=PACK, a=4),
        )

        z_third = sbuf("z_third", [P, QUARTER, PACK], BF16)
        nc.vector.tensor_tensor(
            out=z_third[:],
            in0=high_banks[0][:].rearrange("p t n -> p n t"),
            in1=gain[:].unsqueeze(1).to_broadcast([P, QUARTER, PACK]),
            op=ALU.mult,
        )
        z_last_rows = sbuf("z_last_rows", [P, PACK, QUARTER], BF16)
        z_last = sbuf("z_last", [P, QUARTER, PACK], BF16)
        for t in range(PACK):
            nc.scalar.activation(out=z_last_rows[:, t, :], in_=high_banks[1][:, t, :], func=COPY, scale=gain[:, t : t + 1])
        nc.scalar.copy(out=z_last[:], in_=z_last_rows[:].rearrange("p t n -> p n t"))
        zq = sbuf("zq", [P, S], U32)
        zs = sbuf("zs", [P, S], U8)
        pieces = [(z_low, slice(0, HALF)), (z_third, slice(HALF, HALF + QUARTER)), (z_last, slice(HALF + QUARTER, S))]
        for z, cols in pieces:
            nc.vector.quantize_mx(out=zq[:, cols].bitcast(FP8X4), scales=zs[:, cols], in_=z[:].rearrange("p n t -> p (n t)"))

        out_rows = out.rearrange("(g t a) j -> t g a j", t=PACK, a=4)
        pa, pb, dt = [], [], []

        def second_product(bank_cols, t, cols):
            nc.tensor.matmul_mx(
                out=bank_cols,
                lhsT=cq_dealt[:, P * t : P * (t + 1)].bitcast(FP8X4),
                lhsT_scale=cand_plane[:, P * t : P * (t + 1)],
                rhs=zq[:, cols].bitcast(FP8X4),
                rhs_scale=zs[:, cols],
                start=True,
                stop=True,
            )

        def score_and_fetch(t):
            s = sbuf("s%d" % t, [P, S], F32)
            if t == 0:
                for i, (z, cols) in enumerate(pieces):
                    bank = psum.tile([P, cols.stop - cols.start], F32, name="s_piece%d" % i)
                    second_product(bank[:], t, cols)
                    if i == 0:
                        nc.scalar.activation(out=s[:, cols], in_=bank[:], func=COPY, scale=SIXTEENTH)
                    else:
                        nc.vector.tensor_scalar(out=s[:, cols], in0=bank[:], scalar1=SIXTEENTH, scalar2=None, op0=ALU.mult)
            else:
                bank = psum.tile([P, S], F32, name="s_bank%d" % t, tag="s_bank1" if t == 1 else "h_low%d" % (t - 2))
                second_product(bank[:], t, slice(0, S))
                nc.scalar.activation(out=s[:], in_=bank[:], func=COPY, scale=SIXTEENTH)
            pa.append(sbuf("pa%d" % t, [P, W], F32))
            pb.append(sbuf("pb%d" % t, [P, W], F32))
            if t == 0:
                nc.vector.tensor_copy(pa[t][:], s[:].indirect(n1_sb[:]))
            else:
                nc.scalar.activation(pa[t][:], s[:].indirect(n1_sb[:]), COPY)
            nc.scalar.activation(pb[t][:], s[:].indirect(n2_sb[:]), COPY)
            dt.append(sbuf("dt%d" % t, [P, S], F32))

        def extreme(name, t, op, tag=None):
            tile = sbuf("%s%d" % (name, t), [P, W], F32, tag)
            nc.vector.tensor_tensor(out=tile[:], in0=pa[t][:], in1=pb[t][:], op=op)
            return tile

        def difference(t):
            last = t == PACK - 1
            for h in range(2):
                cols = slice(HALF * h, HALF * (h + 1))
                looked_up = dt[t][:].indirect(n3_sb[:, HALF // 16 * h : HALF // 16 * (h + 1)])
                other = sbuf("other%d_%d" % (t, h), [P, HALF], F32)
                if last and h == 0:
                    nc.vector.tensor_copy(other[:], looked_up)
                else:
                    nc.scalar.activation(other[:], looked_up, COPY)
                result = sbuf("result%d_%d" % (t, h), [P, HALF], F32)
                (nc.vector if last else nc.gpsimd).tensor_tensor(out=result[:], in0=dt[t][:, cols], in1=other[:], op=ALU.subtract)
                nc.sync.dma_start(out=out_rows[t][:, :, cols], in_=result[:])

        for t in range(PACK):
            score_and_fetch(t)
        ra = extreme("ra", 0, ALU.max)
        nc.vector.tensor_copy(dt[0][:].indirect(n1_sb[:]), ra[:])
        for t in range(1, PACK):
            ra = extreme("ra", t, ALU.max)
            rb = extreme("rb", t - 1, ALU.min, "s%d" % t)
            if t == PACK - 1:
                rb_last = extreme("rb", t, ALU.min)
            nc.vector.tensor_copy(dt[t][:].indirect(n1_sb[:]), ra[:])
            nc.vector.tensor_copy(dt[t - 1][:].indirect(n2_sb[:]), rb[:])
            if t == PACK - 1:
                nc.vector.tensor_copy(dt[t][:].indirect(n2_sb[:]), rb_last[:])
            difference(t - 1)
        difference(PACK - 1)
